import numpy as np
import ml_dtypes


def mxq(x, axis, fmt="e4m3"):
    dtype, down = {"e4m3": (ml_dtypes.float8_e4m3fn, 7), "e5m2": (ml_dtypes.float8_e5m2, 14)}[fmt]
    v = np.moveaxis(np.asarray(x, np.float32).astype(ml_dtypes.bfloat16).astype(np.float64), axis, -1)
    blocks = v.reshape(v.shape[:-1] + (-1, 32))
    amax = np.abs(blocks).max(-1, keepdims=True)
    byte = np.maximum(np.where(amax > 0, np.frexp(amax)[1] - 1 + 127, 0) - down, 1)
    scale = np.exp2(byte - 127.0)
    codes = (blocks / scale).astype(np.float32).astype(dtype).astype(np.float64)
    return np.moveaxis((codes * scale).reshape(v.shape), -1, axis)


WIDE = False


def mx_kscale(k):
    if not WIDE:
        return np.ones(k)
    levels = np.array([10, -10, 5, -5, 0])
    if k % 512:
        return np.exp2(np.random.permutation(np.resize(levels, k // 32))).repeat(32)
    a = np.empty((k // 512, 16))
    for p in range(k // 512):
        a[p, :8] = np.random.permutation(np.resize(levels, 8))
        for g in range(8):
            far = levels[np.abs(levels - a[p, g]) >= 10]
            a[p, g + 8] = far[np.random.randint(len(far))]
    return np.exp2(a.ravel()).repeat(32)


def f64(x):
    return np.asarray(x).astype(np.float64)


def striped(idx):
    return np.tile(idx.reshape(-1, 16).T, (8, 1)).astype(np.uint16)


def unstriped(offs):
    return offs[:16].T.reshape(-1).astype(np.int64)


def pack_weight(w):
    k, n = w.shape
    w = f64(np.asarray(w, np.float32).astype(ml_dtypes.bfloat16)).reshape(k // 32, 32, n)
    amax = np.abs(w).max(1)
    byte = np.clip(np.where(amax > 0, np.frexp(amax)[1] - 1 + 127 - 7, 1), 1, 254)
    scaled = (w * np.exp2(127.0 - byte)[:, None, :]).reshape(k, n).astype(np.float32)
    words = np.ascontiguousarray(scaled.reshape(k // 512, 128, 4, n).transpose(0, 1, 3, 2)).astype(ml_dtypes.float8_e4m3fn).view(np.uint8)
    return words, np.ascontiguousarray(byte.astype(np.uint8).reshape(k // 512, 16, n))


def unpack_weight(words, scales):
    g, p, n, _ = words.shape
    vals = np.ascontiguousarray(words).view(ml_dtypes.float8_e4m3fn).astype(np.float64) * np.repeat(np.exp2(scales.astype(np.float64) - 127.0), 8, axis=1)[..., None]
    return vals.transpose(0, 1, 3, 2).reshape(g * 512, n)


K, T, S, D, H, V, Z, W = 512, 2048, 512, 2, 512, 256, 512, 2048
P = 2 ** 7


def setup_inputs():
    n = np.random.standard_normal
    s = mx_kscale(K)[:, None]
    packed_xT = pack_weight(n((K, T)) * s)
    packed_eT = pack_weight(n((K, W)) * s)
    return {
        "x_words": packed_xT[0],
        "x_scales": packed_xT[1],
        "w1": (n((K, H)) / np.sqrt(K) / s).astype(np.float32),
        "e_words": packed_eT[0],
        "e_scales": packed_eT[1],
        "unit": (np.random.uniform(0.6, 1.4, (K, 1)) / np.sqrt(K) / s).astype(np.float32),
        "dst": (np.tile(np.random.uniform(0.2, 1.0, W), (P, 1))).astype(np.float32),
        "offs": striped(np.random.permutation(T)[:S]),
        "plc": striped(np.random.permutation(W)[:Z]),
        "seq": striped(np.random.permutation(V)),
    }


def reference(x_words, x_scales, w1, e_words, e_scales, unit, dst, offs, plc, seq):
    xq = unpack_weight(x_words, x_scales)[:, unstriped(offs)]
    y = mxq(f64(w1), 0, "e4m3").T @ xq
    y2 = (y) ** 2
    ms = y2.mean(axis=1, keepdims=True)
    nd = y / np.sqrt(ms + 0.1)
    sq_ = nd * np.abs(nd)
    agg = sq_.reshape(len(sq_), -1, D).sum(axis=2)
    smo = 0.6 * agg + 0.4 * agg[:, unstriped(seq)]
    hid = f64(unit) * smo
    e_plc = unpack_weight(e_words, e_scales)[:, unstriped(plc)]
    sc = mxq(hid, 0, "e4m3").T @ e_plc
    mu = sc.mean(axis=1, keepdims=True)
    best = sc.max(axis=1, keepdims=True)
    conf = (sc - mu) / (best - mu + 0.3)
    return np.exp(1.0 * np.tanh(conf)) - (f64(dst)[:1][:, unstriped(plc)])

@@ -1,0 +1,186 @@
+from contextlib import ExitStack
+
+import concourse.mybir as mybir
+
+F32 = mybir.dt.float32
+BF16 = mybir.dt.bfloat16
+I32 = mybir.dt.int32
+U32 = mybir.dt.uint32
+U16 = mybir.dt.uint16
+U8 = mybir.dt.uint8
+FP8X4 = mybir.dt.float8_e4m3fn_x4
+ALU = mybir.AluOpType
+ACT = mybir.ActivationFunctionType
+
+P = 128
+PACK = 4
+K, T, S, H, V, Z, W = 512, 2048, 512, 512, 256, 512, 2048
+FLOPS = 2 * K * H * S + 2 * H * V * Z
+
+
+def tile_picked_yplacer_pose_p_kernel(
+    tc, x_words, x_scales, w1, e_words, e_scales, unit, dst, offs, plc, seq, out
+):
+    nc = tc.nc
+    with ExitStack() as ctx:
+        keep = ctx.enter_context(tc.tile_pool(name="keep", bufs=1))
+        psum = ctx.enter_context(tc.psum_pool(name="psum", bufs=1))
+
+        def sb(name, shape, dtype, tag=None):
+            return keep.tile(shape, dtype, name=name, tag=tag or name, align_bytes=64)
+
+        offs_t = sb("offs_t", [P, S // 16], U16)
+        plc_t = sb("plc_t", [P, Z // 16], U16)
+        seq_t = sb("seq_t", [P, V // 16], U16)
+        x_tab = sb("x_tab", [P, T], U32, tag="words")
+        x_sc_tab = sb("x_sc_tab", [P, T], U8)
+        e_sc_tab = sb("e_sc_tab", [P, W], U8)
+        unit_t = sb("unit_t", [P, PACK], F32)
+        w_raw = [sb(f"w_raw{h}", [P, PACK, H // 2], F32) for h in range(2)]
+
+        def load_words(queue, tab, words):
+            queue.dma_start(out=tab[:].bitcast(I32), in_=words[0].rearrange("p n t -> p (n t)").bitcast(I32))
+
+        def load_scales(queue, tab, scales):
+            for r in range(4):
+                queue.dma_start(out=tab[r:P:32, :].bitcast(I32), in_=scales[0, r:16:4, :].bitcast(I32))
+
+        nc.vector.memset(x_sc_tab[:].bitcast(I32), 0)
+        nc.vector.memset(e_sc_tab[:].bitcast(I32), 0)
+        nc.gpsimd.dma_start(out=unit_t[:], in_=unit.rearrange("(p t) o -> p (t o)", t=PACK))
+        nc.sync.dma_start(offs_t[:], offs)
+        load_words(nc.sync, x_tab, x_words)
+        load_scales(nc.sync, x_sc_tab, x_scales)
+        nc.sync.dma_start(plc_t[:], plc)
+        w_rows = w1.rearrange("(p j) c -> p j c", j=PACK)
+        for h in range(2):
+            nc.sync.dma_start(out=w_raw[h][:], in_=w_rows[:, :, h * (H // 2) : (h + 1) * (H // 2)])
+        load_scales(nc.gpsimd, e_sc_tab, e_scales)
+        nc.sync.dma_start(seq_t[:], seq)
+
+        unit_own = sb("unit_own", [P, PACK], F32)
+        nc.scalar.activation(unit_own[:], unit_t[:], ACT.Copy, scale=0.6 * S)
+
+        x_codes = sb("x_codes", [P, S], U32)
+        x_sc = sb("x_sc", [P, S], U8)
+        nc.vector.tensor_copy(x_codes[:], x_tab[:].indirect(offs_t[:]))
+        e_tab = sb("e_tab", [P, W], U32, tag="words")
+        load_words(nc.scalar, e_tab, e_words)
+        nc.vector.tensor_copy(x_sc[:], x_sc_tab[:].indirect(offs_t[:]))
+
+        w_bf = [sb(f"w_bf{u}", [P, 2 * P * PACK], BF16) for u in range(2)]
+        w_codes = [sb(f"w_codes{u}", [P, 2 * P], U32) for u in range(2)]
+        w_sc = [sb(f"w_sc{u}", [P, 2 * P], U8) for u in range(2)]
+
+        def deal_w(copy, h, u):
+            dst_v = w_bf[u][:].rearrange("p (t m j) -> p m j t", t=2, j=PACK)[:, 64 * h : 64 * (h + 1), :, :]
+            src_v = w_raw[h][:].rearrange("p j (m t) -> p m j t", t=PACK)[:, :, :, 2 * u : 2 * u + 2]
+            copy(dst_v, src_v)
+
+        deal_w(nc.scalar.copy, 0, 0)
+        deal_w(nc.scalar.copy, 0, 1)
+        deal_w(nc.vector.tensor_copy, 1, 0)
+        deal_w(nc.scalar.copy, 1, 1)
+        dst_tab = sb("dst_tab", [P, W], F32, tag="w_raw1")
+        nc.sync.dma_start(out=dst_tab[:], in_=dst)
+        for u in range(2):
+            nc.vector.quantize_mx(out=w_codes[u][:].bitcast(FP8X4), scales=w_sc[u][:], in_=w_bf[u][:])
+
+        y = [psum.tile([P, S], F32, name=f"y{t}") for t in range(PACK)]
+        for t in range(PACK):
+            cols = slice(P * (t % 2), P * (t % 2 + 1))
+            nc.tensor.matmul_mx(
+                out=y[t][:],
+                lhsT=w_codes[t // 2][:, cols].bitcast(FP8X4),
+                lhsT_scale=w_sc[t // 2][:, cols],
+                rhs=x_codes[:].bitcast(FP8X4),
+                rhs_scale=x_sc[:],
+                start=True,
+                stop=True,
+            )
+
+        e_sc = sb("e_sc", [P, Z], U8, tag="w_bf0")
+        e_codes = sb("e_codes", [P, Z], U32, tag="w_bf1")
+        nc.vector.tensor_copy(e_sc[:], e_sc_tab[:].indirect(plc_t[:]))
+        nc.vector.tensor_copy(e_codes[:], e_tab[:].indirect(plc_t[:]))
+
+        mag = [sb(f"mag{t}", [P, S], F32) for t in range(PACK)]
+        signed = [sb(f"signed{t}", [P, S], F32) for t in range(PACK)]
+        agg = sb("agg", [P, PACK * V], F32)
+        sumsq = [sb(f"sumsq{u}", [P, 2], F32) for u in range(2)]
+        den = [sb(f"den{u}", [P, 2], F32) for u in range(2)]
+        inv = [sb(f"inv{u}", [P, 2], F32) for u in range(2)]
+        fac = [sb(f"fac{u}", [P, 2], F32) for u in range(2)]
+        for u in range(2):
+            for i in range(2):
+                t = 2 * u + i
+                nc.scalar.activation(mag[t][:], y[t][:], ACT.Square, accum_out=sumsq[u][:, i : i + 1])
+            nc.vector.tensor_scalar(den[u][:], sumsq[u][:], 0.1 * S, None, ALU.add)
+            nc.vector.reciprocal(inv[u][:], den[u][:])
+            nc.vector.tensor_tensor(fac[u][:], inv[u][:], unit_own[:, 2 * u : 2 * u + 2], ALU.mult)
+            for i in range(2):
+                t = 2 * u + i
+                nc.scalar.activation(mag[t][:], y[t][:], ACT.Abs)
+                nc.vector.scalar_tensor_tensor(signed[t][:], y[t][:], fac[u][:, i : i + 1], mag[t][:], ALU.mult, ALU.mult)
+            for i in range(2):
+                t = 2 * u + i
+                adder = nc.vector if t == PACK - 1 else nc.gpsimd
+                adder.tensor_tensor(agg[:, t * V : (t + 1) * V], signed[t][:, 0:S:2], signed[t][:, 1:S:2], ALU.add)
+
+        stats = []
+        for b in range(2):
+            other = sb(f"other{b}", [P, PACK * P], F32)
+            for t in range(PACK):
+                nc.scalar.activation(
+                    other[:, t * P : (t + 1) * P],
+                    agg[:, t * V : (t + 1) * V].indirect(seq_t[:, 8 * b : 8 * (b + 1)]),
+                    ACT.Copy,
+                    scale=0.4 / 0.6,
+                )
+            hid = sb(f"hid{b}", [P, P * PACK], BF16, tag="hid")
+            own = agg[:].rearrange("p (t c i) -> p c t i", t=PACK, i=4)[:, 32 * b : 32 * (b + 1), :, :]
+            nc.vector.tensor_tensor(
+                hid[:].rearrange("p (c i t) -> p c t i", i=4, t=PACK),
+                own,
+                other[:].rearrange("p (t c i) -> p c t i", t=PACK, i=4),
+                ALU.add,
+            )
+            h_codes = sb(f"h_codes{b}", [P, P], U32)
+            h_sc = sb(f"h_sc{b}", [P, P], U8)
+            nc.vector.quantize_mx(out=h_codes[:].bitcast(FP8X4), scales=h_sc[:], in_=hid[:])
+            sc = psum.tile([P, Z], F32, name=f"sc{b}")
+            nc.tensor.matmul_mx(
+                out=sc[:],
+                lhsT=h_codes[:].bitcast(FP8X4),
+                lhsT_scale=h_sc[:],
+                rhs=e_codes[:].bitcast(FP8X4),
+                rhs_scale=e_sc[:],
+                start=True,
+                stop=True,
+            )
+            cen = sb(f"cen{b}", [P, Z], F32)
+            neg_mu = sb(f"neg_mu{b}", [P, 1], F32)
+            top = sb(f"top{b}", [P, 1], F32)
+            span = sb(f"span{b}", [P, 1], F32)
+            inv_span = sb(f"inv_span{b}", [P, 1], F32)
+            nc.scalar.activation(cen[:], sc[:], ACT.Copy, scale=-1.0 / Z, accum_out=neg_mu[:])
+            nc.vector.tensor_scalar(cen[:], sc[:], neg_mu[:], None, ALU.add, ALU.max, accum_out=top[:])
+            nc.vector.tensor_scalar(span[:], top[:], 0.3, None, ALU.add)
+            nc.vector.reciprocal(inv_span[:], span[:])
+            stats.append((cen, inv_span))
+        dst_g = []
+        for q, tag in enumerate(("other1", "span1")):
+            picked = sb(f"dst_g{q}", [P, Z // 2], F32, tag=tag)
+            nc.vector.tensor_copy(picked[:], dst_tab[:].indirect(plc_t[:, 16 * q : 16 * (q + 1)]))
+            dst_g.append(picked)
+        for b in range(2):
+            cen, inv_span = stats[b]
+            squashed = sb(f"squashed{b}", [P, Z], F32)
+            nc.scalar.activation(squashed[:], cen[:], ACT.Tanh, scale=inv_span[:])
+            for q in range(2):
+                cols = slice(q * (Z // 2), (q + 1) * (Z // 2))
+                grown = sb(f"grown{b}{q}", [P, Z // 2], F32)
+                res = sb(f"res{b}{q}", [P, Z // 2], F32)
+                nc.scalar.activation(grown[:], squashed[:, cols], ACT.Exp)
+                nc.vector.tensor_tensor(res[:], grown[:], dst_g[q][:], ALU.subtract)
+                nc.sync.dma_start(out=out[b * P : (b + 1) * P, cols], in_=res[:])

@@ -32,100 +32,116 @@ def tile_picked_yplacer_pose_p_kernel(
         offs_t = sb("offs_t", [P, S // 16], U16)
         plc_t = sb("plc_t", [P, Z // 16], U16)
         seq_t = sb("seq_t", [P, V // 16], U16)
-        x_tab = sb("x_tab", [P, T], U32, tag="words")
+        x_tab = sb("x_tab", [P, T], U32, tag="x_tab")
+        e_tab = sb("e_tab", [P, W], U32, tag="e_tab")
         x_sc_tab = sb("x_sc_tab", [P, T], U8)
         e_sc_tab = sb("e_sc_tab", [P, W], U8)
         unit_t = sb("unit_t", [P, PACK], F32)
-        w_raw = [sb(f"w_raw{h}", [P, PACK, H // 2], F32) for h in range(2)]
+        w_raw = sb("w_raw", [P, PACK, H], F32)
+        dst_tab = sb("dst_tab", [P, W], F32)
 
-        def load_words(queue, tab, words):
-            queue.dma_start(out=tab[:].bitcast(I32), in_=words[0].rearrange("p n t -> p (n t)").bitcast(I32))
+        def load_words(tab, words):
+            nc.sync.dma_start(out=tab[:].bitcast(I32), in_=words[0].rearrange("p n t -> p (n t)").bitcast(I32))
 
         def load_scales(queue, tab, scales):
             for r in range(4):
                 queue.dma_start(out=tab[r:P:32, :].bitcast(I32), in_=scales[0, r:16:4, :].bitcast(I32))
 
         nc.vector.memset(x_sc_tab[:].bitcast(I32), 0)
-        nc.vector.memset(e_sc_tab[:].bitcast(I32), 0)
-        nc.gpsimd.dma_start(out=unit_t[:], in_=unit.rearrange("(p t) o -> p (t o)", t=PACK))
+        nc.gpsimd.memset(e_sc_tab[:].bitcast(I32), 0)
+        nc.sync.dma_start(out=w_raw[:], in_=w1.rearrange("(p j) c -> p j c", j=PACK))
         nc.sync.dma_start(offs_t[:], offs)
-        load_words(nc.sync, x_tab, x_words)
         load_scales(nc.sync, x_sc_tab, x_scales)
+        load_words(x_tab, x_words)
         nc.sync.dma_start(plc_t[:], plc)
-        w_rows = w1.rearrange("(p j) c -> p j c", j=PACK)
-        for h in range(2):
-            nc.sync.dma_start(out=w_raw[h][:], in_=w_rows[:, :, h * (H // 2) : (h + 1) * (H // 2)])
-        load_scales(nc.gpsimd, e_sc_tab, e_scales)
+        load_scales(nc.sync, e_sc_tab, e_scales)
+        nc.sync.dma_start(out=unit_t[:], in_=unit.rearrange("(p t) o -> p (t o)", t=PACK))
+        load_words(e_tab, e_words)
         nc.sync.dma_start(seq_t[:], seq)
-
-        unit_own = sb("unit_own", [P, PACK], F32)
-        nc.scalar.activation(unit_own[:], unit_t[:], ACT.Copy, scale=0.6 * S)
-
-        x_codes = sb("x_codes", [P, S], U32)
-        x_sc = sb("x_sc", [P, S], U8)
-        nc.vector.tensor_copy(x_codes[:], x_tab[:].indirect(offs_t[:]))
-        e_tab = sb("e_tab", [P, W], U32, tag="words")
-        load_words(nc.scalar, e_tab, e_words)
-        nc.vector.tensor_copy(x_sc[:], x_sc_tab[:].indirect(offs_t[:]))
+        nc.sync.dma_start(out=dst_tab[:], in_=dst)
 
         w_bf = [sb(f"w_bf{u}", [P, 2 * P * PACK], BF16) for u in range(2)]
         w_codes = [sb(f"w_codes{u}", [P, 2 * P], U32) for u in range(2)]
-        w_sc = [sb(f"w_sc{u}", [P, 2 * P], U8) for u in range(2)]
+        w_sc = [sb(f"w_sc{u}", [P, 2 * P], U8, tag="x_sc_tab" if u == 0 else None) for u in range(2)]
 
-        def deal_w(copy, h, u):
-            dst_v = w_bf[u][:].rearrange("p (t m j) -> p m j t", t=2, j=PACK)[:, 64 * h : 64 * (h + 1), :, :]
-            src_v = w_raw[h][:].rearrange("p j (m t) -> p m j t", t=PACK)[:, :, :, 2 * u : 2 * u + 2]
-            copy(dst_v, src_v)
+        def deal_w(copy, u, ms):
+            copy(
+                w_bf[u][:].rearrange("p (t m j) -> p m j t", t=2, j=PACK)[:, ms, :, :],
+                w_raw[:].rearrange("p j (m t) -> p m j t", t=PACK)[:, ms, :, 2 * u : 2 * u + 2],
+            )
 
-        deal_w(nc.scalar.copy, 0, 0)
-        deal_w(nc.scalar.copy, 0, 1)
-        deal_w(nc.vector.tensor_copy, 1, 0)
-        deal_w(nc.scalar.copy, 1, 1)
-        dst_tab = sb("dst_tab", [P, W], F32, tag="w_raw1")
-        nc.sync.dma_start(out=dst_tab[:], in_=dst)
+        deal_w(nc.vector.tensor_copy, 1, slice(0, P // 2))
+        deal_w(nc.scalar.copy, 0, slice(0, P))
+        deal_w(nc.scalar.copy, 1, slice(P // 2, P))
+        x_sc = sb("x_sc", [P, S], U8)
+        nc.vector.tensor_copy(x_sc[:], x_sc_tab[:].indirect(offs_t[:]))
         for u in range(2):
             nc.vector.quantize_mx(out=w_codes[u][:].bitcast(FP8X4), scales=w_sc[u][:], in_=w_bf[u][:])
 
+        x_codes = [sb(f"x_codes{h}", [P, S // 2], U32) for h in range(2)]
+        for h in range(2):
+            nc.vector.tensor_copy(x_codes[h][:], x_tab[:].indirect(offs_t[:, 16 * h : 16 * (h + 1)]))
+
         y = [psum.tile([P, S], F32, name=f"y{t}") for t in range(PACK)]
-        for t in range(PACK):
-            cols = slice(P * (t % 2), P * (t % 2 + 1))
-            nc.tensor.matmul_mx(
-                out=y[t][:],
-                lhsT=w_codes[t // 2][:, cols].bitcast(FP8X4),
-                lhsT_scale=w_sc[t // 2][:, cols],
-                rhs=x_codes[:].bitcast(FP8X4),
-                rhs_scale=x_sc[:],
-                start=True,
-                stop=True,
-            )
+        for u in range(2):
+            for h in range(2):
+                for i in range(2):
+                    cols = slice(P * i, P * (i + 1))
+                    picks = slice(h * (S // 2), (h + 1) * (S // 2))
+                    nc.tensor.matmul_mx(
+                        out=y[2 * u + i][:, picks],
+                        lhsT=w_codes[u][:, cols].bitcast(FP8X4),
+                        lhsT_scale=w_sc[u][:, cols],
+                        rhs=x_codes[h][:].bitcast(FP8X4),
+                        rhs_scale=x_sc[:, picks],
+                        start=True,
+                        stop=True,
+                    )
 
-        e_sc = sb("e_sc", [P, Z], U8, tag="w_bf0")
-        e_codes = sb("e_codes", [P, Z], U32, tag="w_bf1")
+        e_sc = sb("e_sc", [P, Z], U8, tag="x_tab")
         nc.vector.tensor_copy(e_sc[:], e_sc_tab[:].indirect(plc_t[:]))
-        nc.vector.tensor_copy(e_codes[:], e_tab[:].indirect(plc_t[:]))
 
+        inv_unit = sb("inv_unit", [P, PACK], F32)
+        nc.vector.reciprocal(inv_unit[:], unit_t[:])
         mag = [sb(f"mag{t}", [P, S], F32) for t in range(PACK)]
         signed = [sb(f"signed{t}", [P, S], F32) for t in range(PACK)]
         agg = sb("agg", [P, PACK * V], F32)
         sumsq = [sb(f"sumsq{u}", [P, 2], F32) for u in range(2)]
-        den = [sb(f"den{u}", [P, 2], F32) for u in range(2)]
-        inv = [sb(f"inv{u}", [P, 2], F32) for u in range(2)]
         fac = [sb(f"fac{u}", [P, 2], F32) for u in range(2)]
-        for u in range(2):
-            for i in range(2):
-                t = 2 * u + i
-                nc.scalar.activation(mag[t][:], y[t][:], ACT.Square, accum_out=sumsq[u][:, i : i + 1])
-            nc.vector.tensor_scalar(den[u][:], sumsq[u][:], 0.1 * S, None, ALU.add)
-            nc.vector.reciprocal(inv[u][:], den[u][:])
-            nc.vector.tensor_tensor(fac[u][:], inv[u][:], unit_own[:, 2 * u : 2 * u + 2], ALU.mult)
-            for i in range(2):
-                t = 2 * u + i
-                nc.scalar.activation(mag[t][:], y[t][:], ACT.Abs)
-                nc.vector.scalar_tensor_tensor(signed[t][:], y[t][:], fac[u][:, i : i + 1], mag[t][:], ALU.mult, ALU.mult)
-            for i in range(2):
-                t = 2 * u + i
-                adder = nc.vector if t == PACK - 1 else nc.gpsimd
-                adder.tensor_tensor(agg[:, t * V : (t + 1) * V], signed[t][:, 0:S:2], signed[t][:, 1:S:2], ALU.add)
+
+        def square(t):
+            nc.scalar.activation(mag[t][:], y[t][:], ACT.Square, accum_out=sumsq[t // 2][:, t % 2 : t % 2 + 1])
+
+        def factor(u, tag):
+            den = sb(f"den{u}", [P, 2], F32, tag=tag)
+            nc.vector.scalar_tensor_tensor(den[:], sumsq[u][:], 0.1 * S, inv_unit[:, 2 * u : 2 * u + 2], ALU.add, ALU.mult)
+            nc.vector.reciprocal(fac[u][:], den[:])
+
+        def signed_square(t):
+            nc.scalar.activation(mag[t][:], y[t][:], ACT.Abs, scale=0.6 * S)
+            nc.vector.scalar_tensor_tensor(
+                signed[t][:], y[t][:], fac[t // 2][:, t % 2 : t % 2 + 1], mag[t][:], ALU.mult, ALU.mult
+            )
+
+        def pair_sum(t):
+            nc.vector.tensor_tensor(agg[:, t * V : (t + 1) * V], signed[t][:, 0:S:2], signed[t][:, 1:S:2], ALU.add)
+
+        square(0)
+        square(1)
+        factor(0, "e_sc_tab")
+        signed_square(0)
+        signed_square(1)
+        pair_sum(0)
+        square(2)
+        square(3)
+        factor(1, "mag1")
+        pair_sum(1)
+        signed_square(2)
+        signed_square(3)
+        pair_sum(2)
+        pair_sum(3)
+        e_codes = sb("e_codes", [P, Z], U32, tag="signed3")
+        nc.vector.tensor_copy(e_codes[:], e_tab[:].indirect(plc_t[:]))
 
         stats = []
         for b in range(2):

from contextlib import ExitStack

import concourse.mybir as mybir

F32 = mybir.dt.float32
BF16 = mybir.dt.bfloat16
I32 = mybir.dt.int32
U32 = mybir.dt.uint32
U16 = mybir.dt.uint16
U8 = mybir.dt.uint8
FP8X4 = mybir.dt.float8_e4m3fn_x4
ALU = mybir.AluOpType
ACT = mybir.ActivationFunctionType

P = 128
PACK = 4
K, T, S, H, V, Z, W = 512, 2048, 512, 512, 256, 512, 2048
FLOPS = 2 * K * H * S + 2 * H * V * Z


def tile_picked_yplacer_pose_p_kernel(
    tc, x_words, x_scales, w1, e_words, e_scales, unit, dst, offs, plc, seq, out
):
    nc = tc.nc
    with ExitStack() as ctx:
        keep = ctx.enter_context(tc.tile_pool(name="keep", bufs=1))
        psum = ctx.enter_context(tc.psum_pool(name="psum", bufs=1))

        def sb(name, shape, dtype, tag=None):
            return keep.tile(shape, dtype, name=name, tag=tag or name, align_bytes=64)

        offs_t = sb("offs_t", [P, S // 16], U16)
        plc_t = sb("plc_t", [P, Z // 16], U16)
        seq_t = sb("seq_t", [P, V // 16], U16)
        x_tab = sb("x_tab", [P, T], U32, tag="x_tab")
        e_tab = sb("e_tab", [P, W], U32, tag="e_tab")
        x_sc_tab = sb("x_sc_tab", [P, T], U8)
        e_sc_tab = sb("e_sc_tab", [P, W], U8)
        unit_t = sb("unit_t", [P, PACK], F32)
        w_raw = sb("w_raw", [P, PACK, H], F32)
        dst_tab = sb("dst_tab", [P, W], F32)

        def load_words(tab, words):
            nc.sync.dma_start(out=tab[:].bitcast(I32), in_=words[0].rearrange("p n t -> p (n t)").bitcast(I32))

        def load_scales(queue, tab, scales):
            for r in range(4):
                queue.dma_start(out=tab[r:P:32, :].bitcast(I32), in_=scales[0, r:16:4, :].bitcast(I32))

        nc.vector.memset(x_sc_tab[:].bitcast(I32), 0)
        nc.gpsimd.memset(e_sc_tab[:].bitcast(I32), 0)
        nc.sync.dma_start(out=w_raw[:], in_=w1.rearrange("(p j) c -> p j c", j=PACK))
        nc.sync.dma_start(offs_t[:], offs)
        load_scales(nc.sync, x_sc_tab, x_scales)
        load_words(x_tab, x_words)
        nc.sync.dma_start(plc_t[:], plc)
        load_scales(nc.sync, e_sc_tab, e_scales)
        nc.sync.dma_start(out=unit_t[:], in_=unit.rearrange("(p t) o -> p (t o)", t=PACK))
        load_words(e_tab, e_words)
        nc.sync.dma_start(seq_t[:], seq)
        nc.sync.dma_start(out=dst_tab[:], in_=dst)

        w_bf = [sb(f"w_bf{u}", [P, 2 * P * PACK], BF16) for u in range(2)]
        w_codes = [sb(f"w_codes{u}", [P, 2 * P], U32) for u in range(2)]
        w_sc = [sb(f"w_sc{u}", [P, 2 * P], U8, tag="x_sc_tab" if u == 0 else None) for u in range(2)]

        def deal_w(copy, u, ms):
            copy(
                w_bf[u][:].rearrange("p (t m j) -> p m j t", t=2, j=PACK)[:, ms, :, :],
                w_raw[:].rearrange("p j (m t) -> p m j t", t=PACK)[:, ms, :, 2 * u : 2 * u + 2],
            )

        deal_w(nc.vector.tensor_copy, 1, slice(0, P // 2))
        deal_w(nc.scalar.copy, 0, slice(0, P))
        deal_w(nc.scalar.copy, 1, slice(P // 2, P))
        x_sc = sb("x_sc", [P, S], U8)
        nc.vector.tensor_copy(x_sc[:], x_sc_tab[:].indirect(offs_t[:]))
        for u in range(2):
            nc.vector.quantize_mx(out=w_codes[u][:].bitcast(FP8X4), scales=w_sc[u][:], in_=w_bf[u][:])

        x_codes = [sb(f"x_codes{h}", [P, S // 2], U32) for h in range(2)]
        for h in range(2):
            nc.vector.tensor_copy(x_codes[h][:], x_tab[:].indirect(offs_t[:, 16 * h : 16 * (h + 1)]))

        y = [psum.tile([P, S], F32, name=f"y{t}") for t in range(PACK)]
        for u in range(2):
            for h in range(2):
                for i in range(2):
                    cols = slice(P * i, P * (i + 1))
                    picks = slice(h * (S // 2), (h + 1) * (S // 2))
                    nc.tensor.matmul_mx(
                        out=y[2 * u + i][:, picks],
                        lhsT=w_codes[u][:, cols].bitcast(FP8X4),
                        lhsT_scale=w_sc[u][:, cols],
                        rhs=x_codes[h][:].bitcast(FP8X4),
                        rhs_scale=x_sc[:, picks],
                        start=True,
                        stop=True,
                    )

        e_sc = sb("e_sc", [P, Z], U8, tag="x_tab")
        nc.vector.tensor_copy(e_sc[:], e_sc_tab[:].indirect(plc_t[:]))

        inv_unit = sb("inv_unit", [P, PACK], F32)
        nc.vector.reciprocal(inv_unit[:], unit_t[:])
        mag = [sb(f"mag{t}", [P, S], F32) for t in range(PACK)]
        signed = [sb(f"signed{t}", [P, S], F32) for t in range(PACK)]
        agg = sb("agg", [P, PACK * V], F32)
        sumsq = [sb(f"sumsq{u}", [P, 2], F32) for u in range(2)]
        fac = [sb(f"fac{u}", [P, 2], F32) for u in range(2)]

        def square(t):
            nc.scalar.activation(mag[t][:], y[t][:], ACT.Square, accum_out=sumsq[t // 2][:, t % 2 : t % 2 + 1])

        def factor(u, tag):
            den = sb(f"den{u}", [P, 2], F32, tag=tag)
            nc.vector.scalar_tensor_tensor(den[:], sumsq[u][:], 0.1 * S, inv_unit[:, 2 * u : 2 * u + 2], ALU.add, ALU.mult)
            nc.vector.reciprocal(fac[u][:], den[:])

        def signed_square(t):
            nc.scalar.activation(mag[t][:], y[t][:], ACT.Abs, scale=0.6 * S)
            nc.vector.scalar_tensor_tensor(
                signed[t][:], y[t][:], fac[t // 2][:, t % 2 : t % 2 + 1], mag[t][:], ALU.mult, ALU.mult
            )

        def pair_sum(t):
            nc.vector.tensor_tensor(agg[:, t * V : (t + 1) * V], signed[t][:, 0:S:2], signed[t][:, 1:S:2], ALU.add)

        square(0)
        square(1)
        factor(0, "e_sc_tab")
        signed_square(0)
        signed_square(1)
        pair_sum(0)
        square(2)
        square(3)
        factor(1, "mag1")
        pair_sum(1)
        signed_square(2)
        signed_square(3)
        pair_sum(2)
        pair_sum(3)
        e_codes = sb("e_codes", [P, Z], U32, tag="signed3")
        nc.vector.tensor_copy(e_codes[:], e_tab[:].indirect(plc_t[:]))

        stats = []
        for b in range(2):
            other = sb(f"other{b}", [P, PACK * P], F32)
            for t in range(PACK):
                nc.scalar.activation(
                    other[:, t * P : (t + 1) * P],
                    agg[:, t * V : (t + 1) * V].indirect(seq_t[:, 8 * b : 8 * (b + 1)]),
                    ACT.Copy,
                    scale=0.4 / 0.6,
                )
            hid = sb(f"hid{b}", [P, P * PACK], BF16, tag="hid")
            own = agg[:].rearrange("p (t c i) -> p c t i", t=PACK, i=4)[:, 32 * b : 32 * (b + 1), :, :]
            nc.vector.tensor_tensor(
                hid[:].rearrange("p (c i t) -> p c t i", i=4, t=PACK),
                own,
                other[:].rearrange("p (t c i) -> p c t i", t=PACK, i=4),
                ALU.add,
            )
            h_codes = sb(f"h_codes{b}", [P, P], U32)
            h_sc = sb(f"h_sc{b}", [P, P], U8)
            nc.vector.quantize_mx(out=h_codes[:].bitcast(FP8X4), scales=h_sc[:], in_=hid[:])
            sc = psum.tile([P, Z], F32, name=f"sc{b}")
            nc.tensor.matmul_mx(
                out=sc[:],
                lhsT=h_codes[:].bitcast(FP8X4),
                lhsT_scale=h_sc[:],
                rhs=e_codes[:].bitcast(FP8X4),
                rhs_scale=e_sc[:],
                start=True,
                stop=True,
            )
            cen = sb(f"cen{b}", [P, Z], F32)
            neg_mu = sb(f"neg_mu{b}", [P, 1], F32)
            top = sb(f"top{b}", [P, 1], F32)
            span = sb(f"span{b}", [P, 1], F32)
            inv_span = sb(f"inv_span{b}", [P, 1], F32)
            nc.scalar.activation(cen[:], sc[:], ACT.Copy, scale=-1.0 / Z, accum_out=neg_mu[:])
            nc.vector.tensor_scalar(cen[:], sc[:], neg_mu[:], None, ALU.add, ALU.max, accum_out=top[:])
            nc.vector.tensor_scalar(span[:], top[:], 0.3, None, ALU.add)
            nc.vector.reciprocal(inv_span[:], span[:])
            stats.append((cen, inv_span))
        dst_g = []
        for q, tag in enumerate(("other1", "span1")):
            picked = sb(f"dst_g{q}", [P, Z // 2], F32, tag=tag)
            nc.vector.tensor_copy(picked[:], dst_tab[:].indirect(plc_t[:, 16 * q : 16 * (q + 1)]))
            dst_g.append(picked)
        for b in range(2):
            cen, inv_span = stats[b]
            squashed = sb(f"squashed{b}", [P, Z], F32)
            nc.scalar.activation(squashed[:], cen[:], ACT.Tanh, scale=inv_span[:])
            for q in range(2):
                cols = slice(q * (Z // 2), (q + 1) * (Z // 2))
                grown = sb(f"grown{b}{q}", [P, Z // 2], F32)
                res = sb(f"res{b}{q}", [P, Z // 2], F32)
                nc.scalar.activation(grown[:], squashed[:, cols], ACT.Exp)
                nc.vector.tensor_tensor(res[:], grown[:], dst_g[q][:], ALU.subtract)
                nc.sync.dma_start(out=out[b * P : (b + 1) * P, cols], in_=res[:])
